import numpy as np, ml_dtypes
CORES = [36,38,116,118,124,126,164,166,244,246,252,254]
N = 12
R, L = 4096, 1024
CAPP = 256
def entries(a): return a.T.reshape(-1)
def pack(v, P): return np.ascontiguousarray(np.asarray(v, np.int32).reshape(-1, P).T)
def lists(rng, how):
    n = N * L
    P = rng.permutation(np.repeat(np.arange(N * N), CAPP))[:n]
    if how == "full":
        a, b = rng.permutation(N)[:2]; o = rng.permutation(N * N); o = o[(o // N != a) & (o % N != b)]
        C = np.concatenate([N * a + rng.permutation(np.delete(np.arange(N), b)), [N * a + b], N * rng.permutation(np.delete(np.arange(N), a)) + b, o])[:n // CAPP]
        P = np.repeat(C, CAPP).reshape(N, L)[rng.permutation(N)].reshape(-1)
    h, g = P // N, P % N
    d = np.zeros(n, np.int64)
    for q in range(N): m = np.nonzero(g == q)[0]; d[m] = R * q + np.concatenate([[0, R - 1], 1 + rng.permutation(R - 2)])[:len(m)]
    s = R * h + rng.integers(0, R, n)
    if how == "fork": s = R * h + rng.integers(0, R, N)[h]
    if how == "chain":
        for q in range(N):
            m = np.nonzero(h == q)[0]; w = d[g == q]
            if len(w): s[m] = w[rng.integers(0, len(w), len(m))]
    if how == "gaps":
        z = rng.permutation(N)[:3]; k = (rng.random(n) < 0.5) | (np.arange(n) // L == z[0]) | (h == z[1]) | (g == z[2]); s[k] = -1; d[k] = -1
    return {"src": np.stack([pack(v, 16) for v in s.reshape(N, L)]), "dst": np.stack([pack(v, 16) for v in d.reshape(N, L)])}
def setup_inputs(rng):
    return dict({"tab": rng.standard_normal((N, 128, R), dtype=np.float32).astype(ml_dtypes.bfloat16)}, **lists(rng, "uniform"))
def setup_inputs_chain(rng):
    d = setup_inputs(rng); d.update(lists(rng, "chain"))
    for k in ("tab",): d[k] = (d[k].astype(np.float32) * 1048576.0).astype(d[k].dtype)
    return d
def setup_inputs_fork(rng):
    d = setup_inputs(rng); d.update(lists(rng, "fork"))
    for k in ("tab",): d[k] = (d[k].astype(np.float32) * (1 / 1024.0)).astype(d[k].dtype)
    return d
def setup_inputs_full(rng):
    d = setup_inputs(rng); d.update(lists(rng, "full"))
    return d
def setup_inputs_gaps(rng):
    d = setup_inputs(rng); d.update(lists(rng, "gaps"))
    return d
def check_inputs(x):
    bad = []; s, d = x["src"].reshape(-1), x["dst"].reshape(-1); k = d >= 0
    if s.min() < -1 or s.max() >= N * R or d.min() < -1 or d.max() >= N * R: bad.append("out of range")
    if ((s < 0) != (d < 0)).any(): bad.append("half a pair")
    if len(np.unique(d[k])) != int(k.sum()): bad.append("a column is written twice")
    if k.any() and int(np.bincount(s[k] // R * N + d[k] // R).max()) > CAPP: bad.append("more than CAPP pairs from one rank's part to one rank's part")
    return bad
def reference(tab, src, dst):
    A = np.concatenate(list(tab), axis=1); Y = A.copy()
    for r in range(N):
        s, d = entries(src[r]), entries(dst[r]); k = d >= 0
        Y[:, d[k]] = A[:, s[k]]
    return {"y": np.stack([Y[:, R * r:R * r + R] for r in range(N)])}

from concourse.bass import DstId, RemoteDMATransfer
from concourse.mybir import dt, AluOpType, AxisListType, ActivationFunctionType

A = AluOpType
COPY = ActivationFunctionType.Copy
NR = 12
R = 4096
CAP = 256
PC = 96
MC = 6
WR = R + 16 * PC
CUTS = [0, 1408, 2688, 4096]
NE = 100


def buffers():
    s = {"ls": ("dram", [NR * 128, 8], "int32"), "ld": ("dram", [NR * 128, 8], "int32")}
    for names, w, t in [
            ("sd ow hl", 2 * PC, "int32"), ("loc", PC, "int32"), ("ip ipm ip7", 1, "int32"),
            ("hlb", 2 * PC, "bfloat16"), ("nm kap ccp", PC, "bfloat16"), ("oh rs zz", NR * PC, "bfloat16"),
            ("ww", WR, "bfloat16"), ("win", R + NR * CAP, "bfloat16"), ("gb", MC * CAP, "bfloat16"),
            ("rb", 4 * CAP, "bfloat16"), ("yb", R, "bfloat16"), ("cone cidw wlo whi cl", 144, "bfloat16"),
            ("cneg ctri", 128, "bfloat16"), ("vs", 16 * PC, "bfloat16"), ("jhi jlo jl0", 256, "bfloat16"),
            ("csid", MC * 128, "bfloat16"), ("crst ccn", 4 * PC, "bfloat16"),
            ("x3 x4 cf cj nmx", PC, "float32"), ("ipf ip7f im ipx mlo mhi cw", 1, "float32"), ("r8 mk", 8, "float32"),
            ("ck cks", MC, "float32"), ("off", PC, "uint16"), ("offs", 16 * MC, "uint16"), ("inv0 inv1 inv2 inv3", 64, "uint16")]:
        for n in names.split():
            s[n] = ("sbuf", [128, w], t)
    for n, w in [("pr", 1536), ("pq", 512), ("pf", 512), ("pe0", 512), ("pe1", 512)]:
        s[n] = ("psum", [128, w], "float32")
    return s


SCRATCH = buffers()
SEMAPHORES = (["sld", "la", "lp", "stile", "stab0", "stab1", "lo", "ll", "lt", "ht", "tpa", "tpb", "da", "st", "ru0", "ru1"]
              + ["e%d" % k for k in range(NE)])


def bits(m):
    return [1 << k for k in range(16) if m >> k & 1]


def same_chip(topo, a, b):
    return topo.host(a) == topo.host(b) and topo.chip(a) == topo.chip(b)


def make_plan(T, topo):
    cores = [int(c) for c in T.cores]
    groups = []
    for i, c in enumerate(cores):
        for gr in groups:
            if same_chip(topo, cores[gr[0]], c):
                gr.append(i)
                break
        else:
            groups.append([i])
    senders, role = {}, {}
    for n, gr in enumerate(groups):
        c0 = cores[gr[0]]
        chip = [c for c in range(c0 - c0 % 8, c0 - c0 % 8 + 8) if same_chip(topo, c, c0)]
        rest = groups[n + 1:] + groups[:n]
        plane = [q for q in rest if topo.same_plane(c0, cores[q[0]])]
        cross = [q for q in rest if q not in plane]
        cross.sort(key=lambda q: topo.mates(c0, cores[q[0]]))
        free = [c for c in chip if c not in cores]

        def owner(c):
            return all(topo.may_write(c, cores[q[0]]) for q in cross)
        here = [c for c in free if topo.die(c) == topo.die(c0)]
        there = [c for c in free if c not in here]
        po, pt = [[c for c in l if owner(c)] for l in (here, there)]
        no, nt = [[c for c in l if not owner(c)] for l in (here, there)]
        plain, port = sorted(gr, key=lambda a: owner(cores[a]))
        if len(cross) > 2:
            senders[plain] = [(pt[0], cross[:2]), (po[0], cross[2:]), (nt[0], plane + [gr])]
            senders[port] = [(nt[1], cross[:2]), (pt[1], cross[2:]), (no[0], plane + [gr])]
        else:
            senders[plain] = [(pt[0], plane[:2]), (po[0], cross), (nt[0], plane[2:] + [gr])]
            senders[port] = [(pt[1], cross), (no[0], plane[:2]), (nt[1], plane[2:] + [gr])]
        for a in gr:
            sl = []
            for c, us in senders[a]:
                sl.append((c, [(None if all(topo.may_write(c, cores[b]) for b in q) else cores[port], q) for q in us]))
            senders[a] = sl
            for s, (c, us) in enumerate(sl):
                role[c] = (a, s, us)
    return cores, groups, senders, role


def dest(topo, d, c):
    rid, pid = topo.addr(d, c)
    return DstId(rid=int(rid), pnc=int(pid))


def constants(g, T, new, m, lists):
    v = g.vector
    fl = {"allow_small_or_imprecise_dtypes": True}
    S = m is not None
    sw = CAP * m if S else R
    nb = 2 if S else 4
    e1, e2, e3, g1, g2, g3 = new(), new(), new(), new(), new(), new()
    h1, h2, h3, h4, h5, h6 = new(), new(), new(), new(), new(), new()
    v.memset(T.cone[:], 1.0).then_inc(e1, 1)
    v.memset(T.cneg[:], -1.0).then_inc(e1, 1)
    v.memset(T.cl[:], 0.0).then_inc(e2, 1)
    v.memset(T.crst[:, 0:nb * PC], 1.0).then_inc(e2, 1)
    g.iota(T.ip[:], [[0, 1]], 0, 1).then_inc(g1, 1)
    g.wait_ge(e1, 2)
    g.affine_select(T.cidw[:], T.cone[:], [[-1, 144]], A.is_equal, 0.0, 8, 1).then_inc(g2, 1)
    g.affine_select(T.ctri[:], T.cneg[:], [[-1, 128]], A.is_ge, 0.0, 0, 1).then_inc(g2, 1)
    lists()
    g.iota(T.r8[:], [[1, 8]], 0, 0, **fl).then_inc(g3, 1)
    if S:
        g.iota(T.ck[:, 0:m], [[CAP, m]], -sw, 0, **fl).then_inc(g3, 1)
        g.iota(T.ccp[:], [[1, PC]], 0, 0, **fl).then_inc(g3, 1)
        n3 = 3
    else:
        g.iota(T.cf[:], [[16, PC]], R, 0, **fl).then_inc(g3, 1)
        g.iota(T.jl0[:], [[0, 16], [16, 16]], 0, 0, **fl).then_inc(g3, 1)
        g.iota(T.jhi[:], [[256, 16], [0, 16]], 0, 0, **fl).then_inc(g3, 1)
        n3 = 4
    v.wait_ge(e2, 2)
    v.memset(T.crst[:, 0:nb * PC:PC], 0.0).then_inc(e3, 1)
    v.memset(T.ww[:, 0:sw + 16 * PC], 0.0).then_inc(e3, 1)
    v.wait_ge(g1, 1)
    v.tensor_scalar(T.ipm[:], T.ip[:], 15, None, A.bitwise_and).then_inc(h1, 1)
    v.tensor_scalar(T.ip7[:], T.ip[:], 7, None, A.bitwise_and).then_inc(h1, 1)
    v.wait_ge(h1, 2)
    v.tensor_copy(T.ipf[:], T.ipm[:]).then_inc(h2, 1)
    v.tensor_copy(T.ip7f[:], T.ip7[:]).then_inc(h2, 1)
    v.tensor_scalar(T.mlo[:], T.ipm[:], 8, None, A.is_lt).then_inc(h2, 1)
    v.tensor_scalar(T.mhi[:], T.ipm[:], 8, None, A.is_ge).then_inc(h2, 1)
    v.wait_ge(h2, 4)
    v.tensor_scalar(T.cw[:], T.mlo[:], 255.0, 1.0, A.mult, A.add).then_inc(h3, 1)
    v.wait_ge(h3, 1)
    v.wait_ge(e1, 2)
    v.tensor_scalar(T.cl[:, 0:144:16], T.cone[:, 0:9], T.cw[:, 0:1], None, A.mult).then_inc(h4, 1)
    v.wait_ge(g2, 2)
    v.tensor_scalar(T.wlo[:], T.cidw[:], T.mlo[:, 0:1], None, A.mult).then_inc(h4, 1)
    v.tensor_scalar(T.whi[:], T.cidw[:], T.mhi[:, 0:1], None, A.mult).then_inc(h4, 1)
    n4, n5, n6 = 4, 0, 0
    v.wait_ge(g3, n3)
    v.tensor_scalar(T.mk[:], T.r8[:], T.ip7f[:, 0:1], None, A.is_equal).then_inc(h4, 1)
    if S:
        v.tensor_scalar(T.im[:], T.ipf[:], -float(PC), None, A.mult).then_inc(h5, 1)
        v.tensor_scalar(T.ipx[:], T.ipf[:], float(PC), float(sw), A.mult, A.add).then_inc(h5, 1)
        for k in range(2):
            v.tensor_scalar(T.ccn[:, PC * k:PC * k + PC], T.ccp[:], -1.0, None, A.mult).then_inc(h5, 1)
        v.wait_ge(h5, 4)
        v.tensor_scalar(T.cks[:, 0:m], T.ck[:, 0:m], T.im[:, 0:1], None, A.add).then_inc(h6, 1)
        v.wait_ge(h6, 1)
        for k in range(m):
            v.tensor_scalar(T.csid[:, 128 * k:128 * k + 128], T.cidw[:, 8:136], T.cks[:, k:k + 1], None,
                            A.mult).then_inc(h6, 1)
        n5, n6 = 4, 1 + m
    else:
        v.tensor_scalar(T.cj[:], T.cf[:], T.ipf[:, 0:1], None, A.add).then_inc(h5, 1)
        v.tensor_scalar(T.jlo[:], T.jl0[:], T.ipf[:, 0:1], None, A.add).then_inc(h5, 1)
        v.wait_ge(h5, 2)
        n5 = 2
    v.wait_ge(h4, n4)
    v.wait_ge(e3, 2)
    for eng in (g.tensor, g.scalar):
        for s, n in ((e1, 2), (g2, 2), (g3, n3), (h4, n4), (h5, n5), (h6, n6)):
            if n:
                eng.wait_ge(s, n)


def put_rows(T, eng, use_v, i, sem, pe):
    o, x, k = T.vs[:, i:16 * PC:16], pe[:, 0:PC], T.mk[:, i % 8:i % 8 + 1]
    if use_v:
        eng.tensor_scalar(o, x, k, None, A.mult).then_inc(sem, 1)
    else:
        eng.activation(o, x, COPY, scale=k).then_inc(sem, 1)


def sender_index(g, T, new, me, classes, ntile):
    v, te, sc = g.vector, g.tensor, g.scalar
    m = len(classes)
    nb = m // 2
    sw = CAP * m
    cid = T.cidw[:, 8:136]
    prs = [T.pr[:, 512 * t:512 * t + 2 * PC] for t in range(nb)]
    pq = T.pq[:, 0:PC]
    for t in range(nb):
        te.matmul(prs[t], cid, T.ccn[:, 0:2 * PC], True, False)
    te.matmul(pq, cid, T.ccp[:], True, False)
    v.wait_ge(T.sem.ht, ntile)
    e1, e2, e3, e4, ee, ex = new(), new(), new(), new(), new(), new()
    v.tensor_scalar(T.hl[:, 0:PC], T.sd[:, 0:PC], 8, 15, A.arith_shift_right, A.bitwise_and).then_inc(e1, 1)
    v.tensor_scalar(T.hl[:, PC:2 * PC], T.sd[:, 0:PC], 255, None, A.bitwise_and).then_inc(e1, 1)
    v.tensor_scalar(T.ow[:], T.sd[:], 12, None, A.arith_shift_right).then_inc(e2, 1)
    v.wait_ge(e1, 2)
    v.tensor_copy(T.hlb[:], T.hl[:]).then_inc(e3, 1)
    v.wait_ge(e2, 1)
    v.tensor_scalar(T.nm[:], T.ow[:, 0:PC], float(me), 64.0, A.not_equal, A.mult).then_inc(e2, 1)
    v.wait_ge(e2, 2)
    v.tensor_tensor(T.kap[:], T.nm[:], T.ow[:, PC:2 * PC], A.add).then_inc(e4, 1)
    v.wait_ge(e4, 1)
    hi, lo = T.hlb[:, 0:PC], T.hlb[:, PC:2 * PC]
    te.wait_ge(e3, 1)
    for pe, w, a, b in ((T.pe1, T.whi, 16, 8), (T.pe0, T.wlo, 8, 0), (T.pf, T.wlo, 8, 0)):
        te.matmul(pe[:, 0:PC], w[:, a:a + 128], hi, True, False)
        te.matmul(pe[:, 0:PC], w[:, b:b + 128], lo, False, True).then_inc(ee, 1)
    sc.wait_ge(ee, 3)
    for i in range(15, 3, -1):
        put_rows(T, sc, False, i, ex, T.pe1 if i >= 8 else T.pe0)
    ep = new()
    er, ez = [new() for _ in range(nb)], [new() for _ in range(nb)]
    for t in range(nb):
        a, b = 2 * PC * t, 2 * PC * t + 2 * PC
        eo, es = new(), new()
        for k in (2 * t, 2 * t + 1):
            v.tensor_scalar(T.oh[:, PC * k:PC * k + PC], T.kap[:], float(classes[k]), None, A.is_equal).then_inc(eo, 1)
        v.wait_ge(eo, 2)
        v.tensor_tensor_scan(T.rs[:, a:b], T.crst[:, 0:2 * PC], T.oh[:, a:b], 0.0, A.mult, A.add).then_inc(es, 1)
        te.wait_ge(eo, 2)
        te.matmul(prs[t], T.ctri[:], T.oh[:, a:b], False, False)
        te.wait_ge(es, 1)
        te.matmul(prs[t], T.cone[:, 0:128], T.rs[:, a:b], False, True).then_inc(er[t], 1)
    for k in range(m):
        te.matmul(pq, T.csid[:, 128 * k:128 * k + 128], T.oh[:, PC * k:PC * k + PC], False, False)
    for t in range(nb):
        a, b = 2 * PC * t, 2 * PC * t + 2 * PC
        v.wait_ge(er[t], 1)
        v.tensor_tensor(T.zz[:, a:b], prs[t], T.oh[:, a:b], A.mult).then_inc(ez[t], 1)
        te.wait_ge(ez[t], 1)
        for k in (2 * t, 2 * t + 1):
            mm = te.matmul(pq, cid, T.zz[:, PC * k:PC * k + PC], False, k == m - 1)
    mm.then_inc(ep, 1)
    v.wait_ge(ee, 3)
    for i in range(4):
        put_rows(T, v, True, i, ex, T.pf)
    q1, q2, q3, q4 = new(), new(), new(), new()
    v.wait_ge(ep, 1)
    v.tensor_scalar(T.off[:], pq, T.ipx[:, 0:1], None, A.add).then_inc(q1, 1)
    v.wait_ge(q1, 1)
    v.wait_ge(ex, 16)
    v.tensor_copy(T.ww[:, 0:sw + 16 * PC].indirect(T.off[:]), T.vs[:]).then_inc(q2, 1)
    te.wait_ge(q2, 1)
    for i in range(16):
        mm = te.matmul(T.pf[:, 0:16 * m], T.cl[:, 16 - i:144 - i], T.ww[:, i:sw:16], i == 0, i == 15)
    mm.then_inc(q3, 1)
    v.wait_ge(q3, 1)
    v.tensor_copy(T.offs[:, 0:16 * m], T.pf[:, 0:16 * m]).then_inc(q4, 1)
    return q4


def receiver_index(g, T, new, me):
    v, te, sc = g.vector, g.tensor, g.scalar
    cid = T.cidw[:, 8:136]
    prs = [T.pr[:, 512 * t:512 * t + 4 * PC] for t in range(3)]
    pq = T.pq[:, 0:PC]
    v.wait_ge(T.sem.stile, 32)
    dst = T.sd[:, PC:2 * PC]
    so, do = T.ow[:, 0:PC], T.ow[:, PC:2 * PC]
    dh, dl = T.hl[:, 0:PC], T.hl[:, PC:2 * PC]
    hi, lo = T.hlb[:, 0:PC], T.hlb[:, PC:2 * PC]
    e1, e2, e3, e4, e5, e6, e7, e8 = [new() for _ in range(8)]
    v.tensor_scalar(T.ow[:], T.sd[:], 12, None, A.arith_shift_right).then_inc(e1, 1)
    v.wait_ge(e1, 1)
    v.tensor_scalar(T.nm[:], do, float(me), 16.0, A.is_equal, A.mult).then_inc(e2, 1)
    v.wait_ge(e2, 1)
    v.tensor_tensor(T.kap[:], T.nm[:], so, A.add).then_inc(e3, 1)
    v.wait_ge(e3, 1)
    eo, es = [new() for _ in range(3)], [new() for _ in range(3)]
    er, ez = [new() for _ in range(3)], [new() for _ in range(3)]

    def masks(t):
        for k in range(4 * t, 4 * t + 4):
            v.tensor_scalar(T.oh[:, PC * k:PC * k + PC], T.kap[:], float(R // CAP + k), None, A.is_equal).then_inc(eo[t], 1)

    def scan(t):
        a, b = 4 * PC * t, 4 * PC * t + 4 * PC
        v.wait_ge(eo[t], 4)
        v.tensor_tensor_scan(T.rs[:, a:b], T.crst[:], T.oh[:, a:b], 0.0, A.mult, A.add).then_inc(es[t], 1)

    def products(t):
        a, b = 4 * PC * t, 4 * PC * t + 4 * PC
        v.wait_ge(er[t], 1)
        v.tensor_tensor(T.zz[:, a:b], prs[t], T.oh[:, a:b], A.mult).then_inc(ez[t], 1)
    for t in range(3):
        masks(t)
        scan(t)
    v.tensor_scalar(dh, dst, 8, 15, A.arith_shift_right, A.bitwise_and).then_inc(e4, 1)
    v.tensor_scalar(dl, dst, 255, None, A.bitwise_and).then_inc(e5, 1)
    products(0)
    v.tensor_scalar(T.loc[:], dst, R - 1, None, A.bitwise_and).then_inc(e6, 1)
    v.tensor_scalar(T.nmx[:], do, float(me), None, A.not_equal).then_inc(e6, 1)
    v.wait_ge(e4, 1)
    v.tensor_tensor(hi, T.kap[:], dh, A.subtract).then_inc(e7, 1)
    products(1)
    v.wait_ge(e6, 2)
    v.tensor_tensor(T.x3[:], T.nmx[:], T.cj[:], A.mult).then_inc(e8, 1)
    products(2)
    q1, q2, q3, q4, ep, ee = [new() for _ in range(6)]
    v.wait_ge(e8, 1)
    v.tensor_tensor(T.x4[:], T.x3[:], T.loc[:], A.max).then_inc(q1, 1)
    v.wait_ge(e5, 1)
    v.wait_ge(ep, 1)
    v.tensor_tensor(lo, pq, dl, A.subtract).then_inc(q2, 1)
    v.wait_ge(q1, 1)
    v.tensor_copy(T.off[:], T.x4[:]).then_inc(q3, 1)
    for t in range(3):
        a, b = 4 * PC * t, 4 * PC * t + 4 * PC
        te.wait_ge(eo[t], 4)
        te.matmul(prs[t], T.ctri[:], T.oh[:, a:b], True, False)
        te.wait_ge(es[t], 1)
        te.matmul(prs[t], T.cone[:, 0:128], T.rs[:, a:b], False, True).then_inc(er[t], 1)
    for t in range(3):
        te.wait_ge(ez[t], 1)
        for k in range(4 * t, 4 * t + 4):
            mm = te.matmul(pq, cid, T.zz[:, PC * k:PC * k + PC], k == 0, k == NR - 1)
    mm.then_inc(ep, 1)
    te.wait_ge(e7, 1)
    te.matmul(T.pe0[:, 0:PC], T.wlo[:, 8:136], hi, True, False)
    te.matmul(T.pe1[:, 0:PC], T.whi[:, 16:144], hi, True, False)
    te.wait_ge(q2, 1)
    te.matmul(T.pe0[:, 0:PC], T.wlo[:, 0:128], lo, False, True).then_inc(ee, 1)
    te.matmul(T.pe1[:, 0:PC], T.whi[:, 8:136], lo, False, True).then_inc(ee, 1)
    ps = [T.pr[:, 0:64], T.pr[:, 512:576], T.pr[:, 1024:1088], T.pf[:, 0:64]]
    for n in range(4):
        te.matmul(ps[n], cid, T.jhi[:, 64 * n:64 * n + 64], True, False)
        te.matmul(ps[n], cid, T.jlo[:, 64 * n:64 * n + 64], False, False)
    ex = new()
    for eng in (v, sc):
        eng.wait_ge(ee, 2)
    for i in range(16):
        put_rows(T, v if i < 8 else sc, i < 8, i, ex, T.pe0 if i < 8 else T.pe1)
    v.wait_ge(ex, 16)
    v.wait_ge(q3, 1)
    v.tensor_copy(T.ww[:].indirect(T.off[:]), T.vs[:]).then_inc(q4, 1)
    te.wait_ge(q4, 1)
    ef = [new() for _ in range(4)]
    for n in range(4):
        for i in range(16):
            mm = te.matmul(ps[n], T.cl[:, 16 - i:144 - i], T.ww[:, 1024 * n + i:1024 * n + 1024:16], False, i == 15)
        mm.then_inc(ef[n], 1)

    def finish(n):
        ed = new()
        v.wait_ge(ef[n], 1)
        v.tensor_copy(T["inv%d" % n][:], ps[n]).then_inc(ed, 1)
        return ed
    return finish


def rank_program(g, core, T, topo):
    cores, groups, senders, role = make_plan(T, topo)
    rank = T.rank_of(core)
    cnt = [0]

    def new():
        cnt[0] += 1
        return T.sem["e%d" % (cnt[0] - 1)]
    if core in role:
        sender_program(g, core, T, topo, new, cores, senders, *role[core])
    elif rank is not None:
        member_program(g, core, T, topo, new, cores, groups, senders, rank)


def block_masks(topo, core, cores, q):
    m = topo.mask(core, cores[q[0]])
    for b in q:
        m &= topo.mask(core, cores[b])
    eb = bits(m)
    n = len(eb) // len(q)
    return [sum(eb[n * j:n * j + n]) for j in range(len(q))]


def send_blocks(g, T, topo, core, cores, a, buf, col, q):
    k = R + CAP * a
    tr = []
    masks = block_masks(topo, core, cores, q)
    for j, b in enumerate(q):
        tr.append(RemoteDMATransfer(srcs=[buf[:, col + CAP * j:col + CAP * j + CAP]], dsts=[T.win[:, k:k + CAP]],
                                    dst_ids=[dest(topo, cores[b], core)], dma_engine_mask=masks[j],
                                    remote_sem=T.sem.da))
    g.remote_dma_fused(tr, local_sem=T.sem.lo)
    return sum(len(bits(m)) for m in masks)


def off_mask(topo, core, cores):
    return [topo.mask(core, c) for c in cores if not same_chip(topo, c, core) and topo.may_write(core, c)][0]


def on_mask(topo, core, c, cores):
    return topo.mask(core, c) & ~off_mask(topo, core, cores)


def send_lists(g, T, topo, core, cores, r, dsts, peer):
    off = bits(off_mask(topo, core, cores))
    tr = []
    rows = slice(128 * r, 128 * r + 128)
    bufs = (T.ls, T.ld)
    for x, buf in enumerate(bufs):
        tr.append(RemoteDMATransfer(srcs=[buf[rows, :]], dsts=[buf[rows, :] for _ in dsts],
                                    dst_ids=[dest(topo, cores[b], core) for b in dsts],
                                    dma_engine_mask=sum(off[4 * x:4 * x + 4]), remote_sem=T.sem.la))
    n = 8
    if peer is not None:
        on = bits(on_mask(topo, core, cores[peer], cores))
        for x, buf in enumerate(bufs):
            tr.append(RemoteDMATransfer(srcs=[buf[rows, :]], dsts=[buf[rows, :]],
                                        dst_ids=[dest(topo, cores[peer], core)],
                                        dma_engine_mask=on[x], remote_sem=T.sem.lp))
        n += 2
    g.remote_dma_fused(tr, local_sem=T.sem.ll)
    return n


def tab_mask(topo, core, cores, sl, s):
    c = sl[s][0]
    return on_mask(topo, core, c, cores) if s == 0 else topo.mask(core, c)


def sender_program(g, core, T, topo, new, cores, senders, a, s, units):
    v, sc = g.vector, g.scalar
    rc = cores[a]
    sl = senders[a]
    classes = [b for _, q in units for b in q]
    constants(g, T, new, len(classes), lambda: None)
    done = sender_index(g, T, new, a, classes, len(bits(topo.mask(rc, core))))
    na = len(bits(tab_mask(topo, rc, cores, sl, s)))
    g.wait_ge(T.sem.tpa, na)
    others = [c for c, _ in sl if c != core]
    x = T.win[:, CUTS[s]:CUTS[s + 1]]
    m = topo.mask(core, others[0])
    g.remote_dma_fused([RemoteDMATransfer(srcs=[x], dsts=[x for _ in others],
                                          dst_ids=[dest(topo, c, core) for c in others], dma_engine_mask=m,
                                          remote_sem=T.sem.tpb)], local_sem=T.sem.lo)
    lo = len(bits(m))
    for eng in (v, sc):
        eng.wait_ge(T.sem.tpa, na)
        eng.wait_ge(T.sem.tpb, sum(len(bits(topo.mask(c, core))) for c in others))
        eng.wait_ge(done, 1)
    for u, (via, q) in enumerate(units):
        eu = new()
        for j in range(2):
            k = 2 * u + j
            i = T.win[:, 0:R].indirect(T.offs[:, 16 * k:16 * k + 16])
            o = T.gb[:, CAP * k:CAP * k + CAP]
            if j:
                v.tensor_copy(o, i).then_inc(eu, 1)
            else:
                sc.activation(o, i, COPY).then_inc(eu, 1)
        g.wait_ge(eu, 2)
        if via is None:
            lo += send_blocks(g, T, topo, core, cores, a, T.gb, 2 * CAP * u, q)
        else:
            m = topo.mask(core, via)
            rid, pid = topo.addr(via, core)
            c0, c1 = 2 * CAP * u, 2 * CAP * u + 2 * CAP
            g.remote_dma(out_ap=T.rb[:, c0:c1], in_ap=T.gb[:, c0:c1], remote_sem=T.sem["ru%d" % u],
                         local_sem=T.sem.lo, pid=pid, routing_id=rid, dma_engine_mask=m)
            lo += len(bits(m))
    g.wait_ge(T.sem.lo, lo)


def member_program(g, core, T, topo, new, cores, groups, senders, rank):
    gr = [q for q in groups if rank in q][0]
    peer = [i for i in gr if i != rank][0]
    outside = [i for q in groups if q is not gr for i in q]
    sl = senders[rank]
    v, sc, sy = g.vector, g.scalar, g.sync
    rows = slice(128 * rank, 128 * rank + 128)
    nla = 8 * len(outside)
    lo, ll = [0], [0]
    left = [b for b in outside if not topo.may_write(cores[peer], cores[b])]
    cs = [c for c, _ in sl]
    mt = topo.mask(core, cs[0])
    sy.dma_start(T.ls[rows, :], T.src[:]).then_inc(T.sem.sld, 16)
    sc.dma_start(T.ld[rows, :], T.dst[:]).then_inc(T.sem.sld, 16)
    sy.dma_start(T.win[:, 0:CUTS[2]], T.tab[:, 0:CUTS[2]]).then_inc(T.sem.stab0, 16)

    def part(s):
        x = T.win[:, CUTS[s]:CUTS[s + 1]]
        m = tab_mask(topo, core, cores, sl, s)
        rid, pid = topo.addr(cs[s], core)
        g.remote_dma(out_ap=x, in_ap=x, remote_sem=T.sem.tpa, local_sem=T.sem.lo, pid=pid, routing_id=rid,
                     dma_engine_mask=m)
        lo[0] += len(bits(m))

    def lists_out():
        g.wait_ge(T.sem.sld, 32)
        ll[0] += send_lists(g, T, topo, core, cores, rank, [b for b in outside if topo.may_write(core, cores[b])], peer)
        g.wait_ge(T.sem.stab0, 16)
        part(0)
        if left:
            g.wait_ge(T.sem.lp, 2)
            ll[0] += send_lists(g, T, topo, core, cores, peer, left, None)
    for eng in (sy, sc):
        eng.wait_ge(T.sem.sld, 32)
        eng.wait_ge(T.sem.lp, 2)
        eng.wait_ge(T.sem.la, nla)
    sy.dma_start(T.sd[:, 0:PC], T.ls[:]).then_inc(T.sem.stile, 16)
    sc.dma_start(T.sd[:, PC:2 * PC], T.ld[:]).then_inc(T.sem.stile, 16)
    constants(g, T, new, None, lists_out)
    finish = receiver_index(g, T, new, rank)
    g.wait_ge(T.sem.stile, 32)
    g.remote_dma_fused([RemoteDMATransfer(srcs=[T.sd[:]], dsts=[T.sd[:] for _ in cs],
                                          dst_ids=[dest(topo, c, core) for c in cs], dma_engine_mask=mt,
                                          remote_sem=T.sem.ht)], local_sem=T.sem.lt)
    part(1)
    sy.wait_ge(T.sem.stile, 32)
    sy.wait_ge(T.sem.lt, len(bits(mt)))
    sy.dma_start(T.win[:, CUTS[2]:R], T.tab[:, CUTS[2]:R]).then_inc(T.sem.stab1, 16)
    g.wait_ge(T.sem.stab1, 16)
    part(2)
    for a in gr:
        for c, us in senders[a]:
            for u, (via, q) in enumerate(us):
                if via == core:
                    g.wait_ge(T.sem["ru%d" % u], len(bits(topo.mask(c, core))))
                    lo[0] += send_blocks(g, T, topo, core, cores, a, T.rb, 2 * CAP * u, q)
    g.wait_ge(T.sem.ll, ll[0])
    g.wait_ge(T.sem.lo, lo[0])
    nda = 0
    for a in range(NR):
        for c, us in senders[a]:
            for via, q in us:
                if rank in q:
                    nda += len(bits(block_masks(topo, c if via is None else via, cores, q)[q.index(rank)]))
    ei = {0: finish(0), 1: finish(1)}
    for eng in (v, sc):
        eng.wait_ge(T.sem.stab0, 16)
        eng.wait_ge(T.sem.stab1, 16)
        eng.wait_ge(T.sem.da, nda)
    nst = 0
    for n in range(4):
        ey = [new(), new()]
        for h, eng in enumerate((v, sc)):
            eng.wait_ge(ei[n], 1)
            c = 1024 * n + 512 * h
            i = T.win[:].indirect(T["inv%d" % n][:, 32 * h:32 * h + 32])
            o = T.yb[:, c:c + 512]
            if h == 0:
                v.tensor_copy(o, i).then_inc(ey[h], 1)
            else:
                sc.activation(o, i, COPY).then_inc(ey[h], 1)
        if n < 2:
            ei[n + 2] = finish(n + 2)
        c = 1024 * n
        for h in range(2):
            sy.wait_ge(ey[h], 1)
            if n == 3:
                sy.dma_start(T.y[:, c + 512 * h:c + 512 * h + 512], T.yb[:, c + 512 * h:c + 512 * h + 512]).then_inc(T.sem.st, 16)
                nst += 16
        if n < 3:
            sy.dma_start(T.y[:, c:c + 1024], T.yb[:, c:c + 1024]).then_inc(T.sem.st, 16)
            nst += 16
    sy.wait_ge(T.sem.st, nst)
